import numpy as np
CORES = [1,126]
N = 2
def setup_inputs(rng):
    return {"x": rng.standard_normal((N, 128, 128), dtype=np.float32)}
def reference(x):
    b = 128 // N
    blocks = x.reshape(N, 128, N, b)
    return {"y": np.ascontiguousarray(blocks.transpose(2, 1, 0, 3)).reshape(N, 128, 128)}

@@ -1,0 +1,52 @@
+from concourse.bass import DstId, RemoteDMATransfer
+
+B = 64
+
+SCRATCH = {
+    "out_full": ("dram", [128, B], "float32"),
+    "in_full": ("dram", [128, B], "float32"),
+    "out_half": ("dram", [2, 128, B // 2], "float32"),
+    "relay": ("dram", [128, B // 2], "float32"),
+    "in_half": ("dram", [2, 128, B // 2], "float32"),
+}
+SEMAPHORES = ["loaded", "sent", "arrived", "stored"]
+
+
+def rank_program(g, core, T, topo):
+    S = T.sem
+    lo, hi = T.cores
+    base = topo.chip(lo) * 8
+    porters = [base + 2, base + 6]
+
+    if core == lo:
+        g.sync.dma_start(T.out_half[:], T.x[:, B:2 * B]).then_inc(S.loaded, 16)
+        g.wait_ge(S.loaded, 16)
+        trs = []
+        for k, p in enumerate(porters):
+            rid, pid, _se = topo.addr(p)
+            trs.append(RemoteDMATransfer(dst_ids=[DstId(rid=rid, pnc=pid)], dma_engine_mask=0xFF << (8 * k),
+                                         remote_sem=S.arrived, src=T.out_half[k], dst=T.relay[:]))
+        g.remote_dma_fused(trs, local_sem=S.sent)
+        g.scalar.wait_ge(S.sent, 16)
+        g.scalar.dma_start(T.y[:, 0:B], T.x[:, 0:B]).then_inc(S.stored, 16)
+        g.sync.wait_ge(S.arrived, 8)
+        g.sync.dma_start(T.y[:, B:2 * B], T.in_full[:]).then_inc(S.stored, 16)
+        g.wait_ge(S.stored, 32)
+
+    elif core in porters:
+        k = porters.index(core)
+        rid, pid, _se = topo.addr(hi)
+        g.wait_ge(S.arrived, 8)
+        g.remote_dma(T.in_half[k], T.relay[:], S.arrived, S.sent, pid, rid, topo.mask(core, hi))
+        g.wait_ge(S.sent, 8)
+
+    elif core == hi:
+        g.sync.dma_start(T.out_full[:], T.x[:, 0:B]).then_inc(S.loaded, 16)
+        g.scalar.dma_start(T.y[:, B:2 * B], T.x[:, B:2 * B]).then_inc(S.stored, 16)
+        g.wait_ge(S.loaded, 16)
+        rid, pid, _se = topo.addr(lo)
+        g.remote_dma(T.in_full[:], T.out_full[:], S.arrived, S.sent, pid, rid, topo.mask(core, lo))
+        g.sync.wait_ge(S.arrived, 16)
+        g.sync.dma_start(T.y[:, 0:B], T.in_half[:]).then_inc(S.stored, 16)
+        g.wait_ge(S.sent, 8)
+        g.wait_ge(S.stored, 32)

@@ -1,15 +1,14 @@
-from concourse.bass import DstId, RemoteDMATransfer
-
 B = 64
+H = B // 2
 
 SCRATCH = {
     "out_full": ("dram", [128, B], "float32"),
     "in_full": ("dram", [128, B], "float32"),
-    "out_half": ("dram", [2, 128, B // 2], "float32"),
-    "relay": ("dram", [128, B // 2], "float32"),
-    "in_half": ("dram", [2, 128, B // 2], "float32"),
+    "out_half": ("dram", [2, 128, H], "float32"),
+    "relay": ("dram", [128, H], "float32"),
+    "in_half": ("dram", [2, 128, H], "float32"),
 }
-SEMAPHORES = ["loaded", "sent", "arrived", "stored"]
+SEMAPHORES = ["loaded", "loaded1", "sent", "arrived", "arrived1", "stored"]
 
 
 def rank_program(g, core, T, topo):
@@ -17,17 +16,17 @@ def rank_program(g, core, T, topo):
     lo, hi = T.cores
     base = topo.chip(lo) * 8
     porters = [base + 2, base + 6]
+    loaded = [S.loaded, S.loaded1]
+    arrived = [S.arrived, S.arrived1]
 
     if core == lo:
-        g.sync.dma_start(T.out_half[:], T.x[:, B:2 * B]).then_inc(S.loaded, 16)
-        g.wait_ge(S.loaded, 16)
-        trs = []
+        g.sync.dma_start(T.out_half[0], T.x[0:64, B:2 * B]).then_inc(loaded[0], 16)
+        g.scalar.dma_start(T.out_half[1], T.x[64:128, B:2 * B]).then_inc(loaded[1], 16)
         for k, p in enumerate(porters):
             rid, pid, _se = topo.addr(p)
-            trs.append(RemoteDMATransfer(dst_ids=[DstId(rid=rid, pnc=pid)], dma_engine_mask=0xFF << (8 * k),
-                                         remote_sem=S.arrived, src=T.out_half[k], dst=T.relay[:]))
-        g.remote_dma_fused(trs, local_sem=S.sent)
-        g.scalar.wait_ge(S.sent, 16)
+            g.wait_ge(loaded[k], 16)
+            g.remote_dma(T.relay[:], T.out_half[k], S.arrived, S.sent, pid, rid, topo.mask(core, p))
+        g.scalar.wait_ge(S.sent, 32)
         g.scalar.dma_start(T.y[:, 0:B], T.x[:, 0:B]).then_inc(S.stored, 16)
         g.sync.wait_ge(S.arrived, 8)
         g.sync.dma_start(T.y[:, B:2 * B], T.in_full[:]).then_inc(S.stored, 16)
@@ -36,8 +35,8 @@ def rank_program(g, core, T, topo):
     elif core in porters:
         k = porters.index(core)
         rid, pid, _se = topo.addr(hi)
-        g.wait_ge(S.arrived, 8)
-        g.remote_dma(T.in_half[k], T.relay[:], S.arrived, S.sent, pid, rid, topo.mask(core, hi))
+        g.wait_ge(S.arrived, 16)
+        g.remote_dma(T.in_half[k], T.relay[:], arrived[k], S.sent, pid, rid, topo.mask(core, hi))
         g.wait_ge(S.sent, 8)
 
     elif core == hi:
@@ -46,7 +45,9 @@ def rank_program(g, core, T, topo):
         g.wait_ge(S.loaded, 16)
         rid, pid, _se = topo.addr(lo)
         g.remote_dma(T.in_full[:], T.out_full[:], S.arrived, S.sent, pid, rid, topo.mask(core, lo))
-        g.sync.wait_ge(S.arrived, 16)
-        g.sync.dma_start(T.y[:, 0:B], T.in_half[:]).then_inc(S.stored, 16)
+        g.sync.wait_ge(arrived[0], 8)
+        g.sync.dma_start(T.y[0:64, 0:B], T.in_half[0]).then_inc(S.stored, 16)
+        g.scalar.wait_ge(arrived[1], 8)
+        g.scalar.dma_start(T.y[64:128, 0:B], T.in_half[1]).then_inc(S.stored, 16)
         g.wait_ge(S.sent, 8)
-        g.wait_ge(S.stored, 32)
+        g.wait_ge(S.stored, 48)

@@ -11,31 +11,37 @@ SCRATCH = {
 SEMAPHORES = ["loaded", "loaded1", "sent", "arrived", "arrived1", "stored"]
 
 
+def engines(mask):
+    return sum((mask >> i) & 1 for i in range(16))
+
+
 def rank_program(g, core, T, topo):
     S = T.sem
     lo, hi = T.cores
-    base = topo.chip(lo) * 8
-    porters = [base + 2, base + 6]
+    relays = [topo.chip(lo) * 8 + 6,
+              (topo.chip(hi) ^ 1) * 8 + 2]
     loaded = [S.loaded, S.loaded1]
     arrived = [S.arrived, S.arrived1]
 
     if core == lo:
         g.sync.dma_start(T.out_half[0], T.x[0:64, B:2 * B]).then_inc(loaded[0], 16)
         g.scalar.dma_start(T.out_half[1], T.x[64:128, B:2 * B]).then_inc(loaded[1], 16)
-        for k, p in enumerate(porters):
+        left = 0
+        for k, p in enumerate(relays):
             rid, pid, _se = topo.addr(p)
             g.wait_ge(loaded[k], 16)
             g.remote_dma(T.relay[:], T.out_half[k], S.arrived, S.sent, pid, rid, topo.mask(core, p))
-        g.scalar.wait_ge(S.sent, 32)
+            left += engines(topo.mask(core, p))
+        g.scalar.wait_ge(S.sent, left)
         g.scalar.dma_start(T.y[:, 0:B], T.x[:, 0:B]).then_inc(S.stored, 16)
         g.sync.wait_ge(S.arrived, 8)
         g.sync.dma_start(T.y[:, B:2 * B], T.in_full[:]).then_inc(S.stored, 16)
         g.wait_ge(S.stored, 32)
 
-    elif core in porters:
-        k = porters.index(core)
+    elif core in relays:
+        k = relays.index(core)
         rid, pid, _se = topo.addr(hi)
-        g.wait_ge(S.arrived, 16)
+        g.wait_ge(S.arrived, engines(topo.mask(lo, core)))
         g.remote_dma(T.in_half[k], T.relay[:], arrived[k], S.sent, pid, rid, topo.mask(core, hi))
         g.wait_ge(S.sent, 8)
 

B = 64
H = B // 2

SCRATCH = {
    "out_full": ("dram", [128, B], "float32"),
    "in_full": ("dram", [128, B], "float32"),
    "out_half": ("dram", [2, 128, H], "float32"),
    "relay": ("dram", [128, H], "float32"),
    "in_half": ("dram", [2, 128, H], "float32"),
}
SEMAPHORES = ["loaded", "loaded1", "sent", "arrived", "arrived1", "stored"]


def engines(mask):
    return sum((mask >> i) & 1 for i in range(16))


def rank_program(g, core, T, topo):
    S = T.sem
    lo, hi = T.cores
    relays = [topo.chip(lo) * 8 + 6,
              (topo.chip(hi) ^ 1) * 8 + 2]
    loaded = [S.loaded, S.loaded1]
    arrived = [S.arrived, S.arrived1]

    if core == lo:
        g.sync.dma_start(T.out_half[0], T.x[0:64, B:2 * B]).then_inc(loaded[0], 16)
        g.scalar.dma_start(T.out_half[1], T.x[64:128, B:2 * B]).then_inc(loaded[1], 16)
        left = 0
        for k, p in enumerate(relays):
            rid, pid, _se = topo.addr(p)
            g.wait_ge(loaded[k], 16)
            g.remote_dma(T.relay[:], T.out_half[k], S.arrived, S.sent, pid, rid, topo.mask(core, p))
            left += engines(topo.mask(core, p))
        g.scalar.wait_ge(S.sent, left)
        g.scalar.dma_start(T.y[:, 0:B], T.x[:, 0:B]).then_inc(S.stored, 16)
        g.sync.wait_ge(S.arrived, 8)
        g.sync.dma_start(T.y[:, B:2 * B], T.in_full[:]).then_inc(S.stored, 16)
        g.wait_ge(S.stored, 32)

    elif core in relays:
        k = relays.index(core)
        rid, pid, _se = topo.addr(hi)
        g.wait_ge(S.arrived, engines(topo.mask(lo, core)))
        g.remote_dma(T.in_half[k], T.relay[:], arrived[k], S.sent, pid, rid, topo.mask(core, hi))
        g.wait_ge(S.sent, 8)

    elif core == hi:
        g.sync.dma_start(T.out_full[:], T.x[:, 0:B]).then_inc(S.loaded, 16)
        g.scalar.dma_start(T.y[:, B:2 * B], T.x[:, B:2 * B]).then_inc(S.stored, 16)
        g.wait_ge(S.loaded, 16)
        rid, pid, _se = topo.addr(lo)
        g.remote_dma(T.in_full[:], T.out_full[:], S.arrived, S.sent, pid, rid, topo.mask(core, lo))
        g.sync.wait_ge(arrived[0], 8)
        g.sync.dma_start(T.y[0:64, 0:B], T.in_half[0]).then_inc(S.stored, 16)
        g.scalar.wait_ge(arrived[1], 8)
        g.scalar.dma_start(T.y[64:128, 0:B], T.in_half[1]).then_inc(S.stored, 16)
        g.wait_ge(S.sent, 8)
        g.wait_ge(S.stored, 48)
